import numpy as np
CORES = [2,10,18,26]
N = 4
ROUNDS = 4
def setup_inputs(rng):
    return {"x": rng.standard_normal((N, ROUNDS, 128, 256), dtype=np.float32)}
def reference(x):
    s = x.sum(axis=0, dtype=np.float64).astype(x.dtype)
    return {"y": np.broadcast_to(s, (N,) + s.shape)}

@@ -1,0 +1,127 @@
+import concourse.bass as bass
+
+S = 2
+W = 64
+SCRATCH = {
+    "stg": ("dram", [S * 4, 128, W], "float32"),
+    "land": ("dram", [S * 3, 128, W], "float32"),
+    "back": ("dram", [S, 128, W], "float32"),
+}
+SEMAPHORES = (
+    ["%s%d" % (n, u) for n in ("ld", "cp", "co", "rs", "bn", "sn", "fs", "cr") for u in range(4)]
+    + ["ag%d%d" % (q, u) for q in range(4) for u in range(4)]
+)
+
+
+def rank_program(g, core, T, topo):
+    r = T.rank_of(core)
+    if r is None:
+        return
+    cores = T.cores
+    sm = T.sem
+    LD = [sm.ld0, sm.ld1, sm.ld2, sm.ld3]
+    CP = [sm.cp0, sm.cp1, sm.cp2, sm.cp3]
+    CO = [sm.co0, sm.co1, sm.co2, sm.co3]
+    RS = [sm.rs0, sm.rs1, sm.rs2, sm.rs3]
+    BN = [sm.bn0, sm.bn1, sm.bn2, sm.bn3]
+    SN = [sm.sn0, sm.sn1, sm.sn2, sm.sn3]
+    FS = [sm.fs0, sm.fs1, sm.fs2, sm.fs3]
+    CR = [sm.cr0, sm.cr1, sm.cr2, sm.cr3]
+    AG = [[sm.ag00, sm.ag01, sm.ag02, sm.ag03], [sm.ag10, sm.ag11, sm.ag12, sm.ag13],
+          [sm.ag20, sm.ag21, sm.ag22, sm.ag23], [sm.ag30, sm.ag31, sm.ag32, sm.ag33]]
+
+    my_chip = topo.chip(core)
+    mate = [q for q in range(4) if topo.mates(my_chip, topo.chip(cores[q]))][0]
+    plane = [q for q in range(4) if topo.same_plane(my_chip, topo.chip(cores[q]))][0]
+    diag = [q for q in range(4) if q not in (r, mate, plane)][0]
+    others = [mate, plane, diag]
+
+    def dst(q):
+        a = topo.addr(cores[q])
+        return bass.DstId(rid=a[0], pnc=a[1])
+
+    def lidx(sender, receiver):
+        return sender if sender < receiver else sender - 1
+
+    def rows(t, u, q0, q1):
+        if len(t.shape) == 3:
+            return t[u, 32 * q0:32 * q1, :]
+        return t[128 * u + 32 * q0:128 * u + 32 * q1, :]
+
+    def load(u):
+        s = u % S
+        g.dma_start(T.stg[4 * s:4 * s + 4], rows(T.x, u, 0, 4)).then_inc(LD[u], 16)
+
+    def scatter(u):
+        s = u % S
+        tr = []
+        for q, m in ((mate, 0x03), (diag, 0x0C), (plane, 0xF0)):
+            tr.append(bass.RemoteDMATransfer(dst_ids=[dst(q)], dma_engine_mask=m, remote_sem=RS[u],
+                                             src=T.stg[4 * s + q], dst=T.land[3 * s + lidx(r, q)]))
+        g.remote_dma_fused(tr, local_sem=SN[u])
+
+    def fold(u):
+        s = u % S
+        tr = bass.RemoteDMATransfer(dst_ids=[dst(q) for q in others], dma_engine_mask=0xFF, remote_sem=AG[r][u],
+                                    srcs=[T.stg[4 * s + r], T.land[3 * s], T.land[3 * s + 1], T.land[3 * s + 2]],
+                                    dsts=[T.stg[4 * s + r] for q in others], alu_op=1)
+        g.remote_dma_fused([tr], local_sem=FS[u])
+
+    def give_back(u):
+        s = u % S
+        a = topo.addr(cores[mate])
+        g.remote_dma(T.back[s], T.stg[4 * s + mate], BN[u], SN[u], a[1], a[0], 0xFF)
+
+    def credit(u):
+        tr = [bass.RemoteDMATransfer(dst_ids=[dst(q)], dma_engine_mask=1 << i, remote_sem=CR[u + S])
+              for i, q in enumerate(others)]
+        g.remote_dma_fused(tr, local_sem=SN[u])
+
+    def store_others(u):
+        s = u % S
+        n = 0
+        for q0, q1 in ((0, r), (r + 1, 4)):
+            if q1 > q0:
+                g.dma_start(rows(T.y, u, q0, q1), T.stg[4 * s + q0:4 * s + q1]).then_inc(CP[u], 16)
+                n += 16
+        return n
+
+    def store_own(u):
+        g.dma_start(rows(T.y, u, r, r + 1), T.back[u % S]).then_inc(CO[u], 16)
+
+    ncp = 16 if r in (0, 3) else 32
+    for b in range(0, 4, S):
+        batch = range(b, b + S)
+        for u in batch:
+            if u >= S:
+                g.wait_ge(CP[u - S], ncp)
+                g.wait_ge(SN[u - S], 19)
+            load(u)
+        for u in batch:
+            g.wait_ge(LD[u], 16)
+            if u >= S:
+                g.wait_ge(CR[u], 3)
+            scatter(u)
+        for u in batch:
+            g.wait_ge(RS[u], 8)
+            if u >= S:
+                g.wait_ge(CO[u - S], 16)
+            fold(u)
+        for u in batch:
+            g.wait_ge(AG[mate][u], 8)
+            give_back(u)
+        for u in batch:
+            g.wait_ge(FS[u], 8)
+            if u + S < 4:
+                credit(u)
+        for u in batch:
+            g.wait_ge(AG[plane][u], 8)
+            g.wait_ge(AG[diag][u], 8)
+            store_others(u)
+        for u in batch:
+            g.wait_ge(BN[u], 8)
+            store_own(u)
+    for u in range(4 - S, 4):
+        g.wait_ge(CP[u], ncp)
+        g.wait_ge(CO[u], 16)
+        g.wait_ge(SN[u], 16)

@@ -1,16 +1,12 @@
 import concourse.bass as bass
 
-S = 2
-W = 64
+W = 128
 SCRATCH = {
-    "stg": ("dram", [S * 4, 128, W], "float32"),
-    "land": ("dram", [S * 3, 128, W], "float32"),
-    "back": ("dram", [S, 128, W], "float32"),
+    "stg": ("dram", [4, 128, W], "float32"),
+    "land": ("dram", [3, 128, W], "float32"),
+    "back": ("dram", [128, W], "float32"),
 }
-SEMAPHORES = (
-    ["%s%d" % (n, u) for n in ("ld", "cp", "co", "rs", "bn", "sn", "fs", "cr") for u in range(4)]
-    + ["ag%d%d" % (q, u) for q in range(4) for u in range(4)]
-)
+SEMAPHORES = ["ld", "cp", "co", "rs", "bn", "sn", "fs", "cr", "ag0", "ag1", "ag2", "ag3"]
 
 
 def rank_program(g, core, T, topo):
@@ -19,16 +15,7 @@ def rank_program(g, core, T, topo):
         return
     cores = T.cores
     sm = T.sem
-    LD = [sm.ld0, sm.ld1, sm.ld2, sm.ld3]
-    CP = [sm.cp0, sm.cp1, sm.cp2, sm.cp3]
-    CO = [sm.co0, sm.co1, sm.co2, sm.co3]
-    RS = [sm.rs0, sm.rs1, sm.rs2, sm.rs3]
-    BN = [sm.bn0, sm.bn1, sm.bn2, sm.bn3]
-    SN = [sm.sn0, sm.sn1, sm.sn2, sm.sn3]
-    FS = [sm.fs0, sm.fs1, sm.fs2, sm.fs3]
-    CR = [sm.cr0, sm.cr1, sm.cr2, sm.cr3]
-    AG = [[sm.ag00, sm.ag01, sm.ag02, sm.ag03], [sm.ag10, sm.ag11, sm.ag12, sm.ag13],
-          [sm.ag20, sm.ag21, sm.ag22, sm.ag23], [sm.ag30, sm.ag31, sm.ag32, sm.ag33]]
+    AG = [sm.ag0, sm.ag1, sm.ag2, sm.ag3]
 
     my_chip = topo.chip(core)
     mate = [q for q in range(4) if topo.mates(my_chip, topo.chip(cores[q]))][0]
@@ -43,85 +30,80 @@ def rank_program(g, core, T, topo):
     def lidx(sender, receiver):
         return sender if sender < receiver else sender - 1
 
-    def rows(t, u, q0, q1):
-        if len(t.shape) == 3:
-            return t[u, 32 * q0:32 * q1, :]
-        return t[128 * u + 32 * q0:128 * u + 32 * q1, :]
+    def spans(t, u, q0, q1):
+        if len(t.shape) == 2:
+            return [(q0, q1, t[256 * u + 64 * q0:256 * u + 64 * q1, :])]
+        if (q0, q1) == (0, 4):
+            return [(0, 4, t[2 * u:2 * u + 2])]
+        out = []
+        for k in range(2):
+            a, b = max(q0, 2 * k), min(q1, 2 * k + 2)
+            if b > a:
+                out.append((a, b, t[2 * u + k, 64 * (a - 2 * k):64 * (b - 2 * k), :]))
+        return out
 
     def load(u):
-        s = u % S
-        g.dma_start(T.stg[4 * s:4 * s + 4], rows(T.x, u, 0, 4)).then_inc(LD[u], 16)
+        g.dma_start(T.stg[0:4], spans(T.x, u, 0, 4)[0][2]).then_inc(sm.ld, 16)
 
-    def scatter(u):
-        s = u % S
+    def scatter():
         tr = []
         for q, m in ((mate, 0x03), (diag, 0x0C), (plane, 0xF0)):
-            tr.append(bass.RemoteDMATransfer(dst_ids=[dst(q)], dma_engine_mask=m, remote_sem=RS[u],
-                                             src=T.stg[4 * s + q], dst=T.land[3 * s + lidx(r, q)]))
-        g.remote_dma_fused(tr, local_sem=SN[u])
+            tr.append(bass.RemoteDMATransfer(dst_ids=[dst(q)], dma_engine_mask=m, remote_sem=sm.rs,
+                                             src=T.stg[q], dst=T.land[lidx(r, q)]))
+        g.remote_dma_fused(tr, local_sem=sm.sn)
 
-    def fold(u):
-        s = u % S
-        tr = bass.RemoteDMATransfer(dst_ids=[dst(q) for q in others], dma_engine_mask=0xFF, remote_sem=AG[r][u],
-                                    srcs=[T.stg[4 * s + r], T.land[3 * s], T.land[3 * s + 1], T.land[3 * s + 2]],
-                                    dsts=[T.stg[4 * s + r] for q in others], alu_op=1)
-        g.remote_dma_fused([tr], local_sem=FS[u])
+    def fold():
+        tr = bass.RemoteDMATransfer(dst_ids=[dst(q) for q in others], dma_engine_mask=0xFF, remote_sem=AG[r],
+                                    srcs=[T.stg[r], T.land[0], T.land[1], T.land[2]],
+                                    dsts=[T.stg[r] for q in others], alu_op=1)
+        g.remote_dma_fused([tr], local_sem=sm.fs)
 
-    def give_back(u):
-        s = u % S
+    def give_back():
         a = topo.addr(cores[mate])
-        g.remote_dma(T.back[s], T.stg[4 * s + mate], BN[u], SN[u], a[1], a[0], 0xFF)
+        g.remote_dma(T.back[:], T.stg[mate], sm.bn, sm.sn, a[1], a[0], 0xFF)
 
-    def credit(u):
-        tr = [bass.RemoteDMATransfer(dst_ids=[dst(q)], dma_engine_mask=1 << i, remote_sem=CR[u + S])
+    def credit():
+        tr = [bass.RemoteDMATransfer(dst_ids=[dst(q)], dma_engine_mask=1 << i, remote_sem=sm.cr)
               for i, q in enumerate(others)]
-        g.remote_dma_fused(tr, local_sem=SN[u])
+        g.remote_dma_fused(tr, local_sem=sm.sn)
 
     def store_others(u):
-        s = u % S
         n = 0
         for q0, q1 in ((0, r), (r + 1, 4)):
             if q1 > q0:
-                g.dma_start(rows(T.y, u, q0, q1), T.stg[4 * s + q0:4 * s + q1]).then_inc(CP[u], 16)
-                n += 16
+                for a, b, ap in spans(T.y, u, q0, q1):
+                    g.dma_start(ap, T.stg[a:b]).then_inc(sm.cp, 16)
+                    n += 16
         return n
 
     def store_own(u):
-        g.dma_start(rows(T.y, u, r, r + 1), T.back[u % S]).then_inc(CO[u], 16)
+        g.dma_start(spans(T.y, u, r, r + 1)[0][2], T.back[:]).then_inc(sm.co, 16)
 
-    ncp = 16 if r in (0, 3) else 32
-    for b in range(0, 4, S):
-        batch = range(b, b + S)
-        for u in batch:
-            if u >= S:
-                g.wait_ge(CP[u - S], ncp)
-                g.wait_ge(SN[u - S], 19)
-            load(u)
-        for u in batch:
-            g.wait_ge(LD[u], 16)
-            if u >= S:
-                g.wait_ge(CR[u], 3)
-            scatter(u)
-        for u in batch:
-            g.wait_ge(RS[u], 8)
-            if u >= S:
-                g.wait_ge(CO[u - S], 16)
-            fold(u)
-        for u in batch:
-            g.wait_ge(AG[mate][u], 8)
-            give_back(u)
-        for u in batch:
-            g.wait_ge(FS[u], 8)
-            if u + S < 4:
-                credit(u)
-        for u in batch:
-            g.wait_ge(AG[plane][u], 8)
-            g.wait_ge(AG[diag][u], 8)
-            store_others(u)
-        for u in batch:
-            g.wait_ge(BN[u], 8)
-            store_own(u)
-    for u in range(4 - S, 4):
-        g.wait_ge(CP[u], ncp)
-        g.wait_ge(CO[u], 16)
-        g.wait_ge(SN[u], 16)
+    ncp = 0
+    load(0)
+    for u in range(2):
+        n = u + 1
+        g.wait_ge(sm.ld, 16 * n)
+        if u:
+            g.wait_ge(sm.cr, 3)
+        scatter()
+        g.wait_ge(sm.rs, 8 * n)
+        if u:
+            g.wait_ge(sm.co, 16)
+        fold()
+        g.wait_ge(AG[mate], 8 * n)
+        give_back()
+        g.wait_ge(AG[plane], 8 * n)
+        g.wait_ge(AG[diag], 8 * n)
+        ncp += store_others(u)
+        g.wait_ge(sm.fs, 8 * n)
+        if u == 0:
+            credit()
+            g.wait_ge(sm.cp, ncp)
+            g.wait_ge(sm.sn, 19)
+            load(1)
+        g.wait_ge(sm.bn, 8 * n)
+        store_own(u)
+    g.wait_ge(sm.cp, ncp)
+    g.wait_ge(sm.co, 32)
+    g.wait_ge(sm.sn, 19 + 16)

@@ -1,12 +1,13 @@
 import concourse.bass as bass
+from concourse.mybir import AluOpType
 
 W = 128
 SCRATCH = {
     "stg": ("dram", [4, 128, W], "float32"),
     "land": ("dram", [3, 128, W], "float32"),
-    "back": ("dram", [128, W], "float32"),
+    "dup": ("dram", [128, W], "float32"),
 }
-SEMAPHORES = ["ld", "cp", "co", "rs", "bn", "sn", "fs", "cr", "ag0", "ag1", "ag2", "ag3"]
+SEMAPHORES = ["ld", "yo", "aa", "a3", "cp", "rs", "sn", "fs", "cr", "ag"]
 
 
 def rank_program(g, core, T, topo):
@@ -15,7 +16,6 @@ def rank_program(g, core, T, topo):
         return
     cores = T.cores
     sm = T.sem
-    AG = [sm.ag0, sm.ag1, sm.ag2, sm.ag3]
 
     my_chip = topo.chip(core)
     mate = [q for q in range(4) if topo.mates(my_chip, topo.chip(cores[q]))][0]
@@ -42,30 +42,33 @@ def rank_program(g, core, T, topo):
                 out.append((a, b, t[2 * u + k, 64 * (a - 2 * k):64 * (b - 2 * k), :]))
         return out
 
+    def own(t, u):
+        return spans(t, u, r, r + 1)[0][2]
+
     def load(u):
         g.dma_start(T.stg[0:4], spans(T.x, u, 0, 4)[0][2]).then_inc(sm.ld, 16)
 
     def scatter():
         tr = []
-        for q, m in ((mate, 0x03), (diag, 0x0C), (plane, 0xF0)):
+        for q, m, d in ((diag, 0x03, T.land[lidx(r, diag)]), (mate, 0x0C, T.land[lidx(r, mate)]),
+                        (plane, 0x30, T.land[lidx(r, plane)]), (plane, 0xC0, T.dup[:])):
             tr.append(bass.RemoteDMATransfer(dst_ids=[dst(q)], dma_engine_mask=m, remote_sem=sm.rs,
-                                             src=T.stg[q], dst=T.land[lidx(r, q)]))
+                                             src=T.stg[q], dst=d))
         g.remote_dma_fused(tr, local_sem=sm.sn)
 
     def fold():
-        tr = bass.RemoteDMATransfer(dst_ids=[dst(q) for q in others], dma_engine_mask=0xFF, remote_sem=AG[r],
+        tr = bass.RemoteDMATransfer(dst_ids=[dst(q) for q in others], dma_engine_mask=0xFF, remote_sem=sm.ag,
                                     srcs=[T.stg[r], T.land[0], T.land[1], T.land[2]],
                                     dsts=[T.stg[r] for q in others], alu_op=1)
         g.remote_dma_fused([tr], local_sem=sm.fs)
-
-    def give_back():
-        a = topo.addr(cores[mate])
-        g.remote_dma(T.back[:], T.stg[mate], sm.bn, sm.sn, a[1], a[0], 0xFF)
 
     def credit():
         tr = [bass.RemoteDMATransfer(dst_ids=[dst(q)], dma_engine_mask=1 << i, remote_sem=sm.cr)
               for i, q in enumerate(others)]
         g.remote_dma_fused(tr, local_sem=sm.sn)
+
+    def add(out, in_, sem):
+        g.dma_start(out, in_, accum_op=AluOpType.add, max_dma_last_dim=8192).then_inc(sem, 16)
 
     def store_others(u):
         n = 0
@@ -76,34 +79,32 @@ def rank_program(g, core, T, topo):
                     n += 16
         return n
 
-    def store_own(u):
-        g.dma_start(spans(T.y, u, r, r + 1)[0][2], T.back[:]).then_inc(sm.co, 16)
-
     ncp = 0
     load(0)
+    for u in range(2):
+        g.dma_start(own(T.y, u), own(T.x, u)).then_inc(sm.yo, 16)
     for u in range(2):
         n = u + 1
         g.wait_ge(sm.ld, 16 * n)
         if u:
             g.wait_ge(sm.cr, 3)
         scatter()
+        if u == 0:
+            g.wait_ge(sm.yo, 32)
         g.wait_ge(sm.rs, 8 * n)
-        if u:
-            g.wait_ge(sm.co, 16)
         fold()
-        g.wait_ge(AG[mate], 8 * n)
-        give_back()
-        g.wait_ge(AG[plane], 8 * n)
-        g.wait_ge(AG[diag], 8 * n)
+        add(own(T.y, u), T.land[lidx(mate, r)], sm.aa)
+        add(T.dup[:], T.land[lidx(diag, r)], sm.aa)
+        g.wait_ge(sm.aa, 32 * n)
+        add(own(T.y, u), T.dup[:], sm.a3)
+        g.wait_ge(sm.ag, 24 * n)
         ncp += store_others(u)
         g.wait_ge(sm.fs, 8 * n)
+        g.wait_ge(sm.a3, 16 * n)
         if u == 0:
             credit()
             g.wait_ge(sm.cp, ncp)
-            g.wait_ge(sm.sn, 19)
+            g.wait_ge(sm.sn, 11)
             load(1)
-        g.wait_ge(sm.bn, 8 * n)
-        store_own(u)
     g.wait_ge(sm.cp, ncp)
-    g.wait_ge(sm.co, 32)
-    g.wait_ge(sm.sn, 19 + 16)
+    g.wait_ge(sm.sn, 19)

import concourse.bass as bass
from concourse.mybir import AluOpType

W = 128
SCRATCH = {
    "stg": ("dram", [4, 128, W], "float32"),
    "land": ("dram", [3, 128, W], "float32"),
    "dup": ("dram", [128, W], "float32"),
}
SEMAPHORES = ["ld", "yo", "aa", "a3", "cp", "rs", "sn", "fs", "cr", "ag"]


def rank_program(g, core, T, topo):
    r = T.rank_of(core)
    if r is None:
        return
    cores = T.cores
    sm = T.sem

    my_chip = topo.chip(core)
    mate = [q for q in range(4) if topo.mates(my_chip, topo.chip(cores[q]))][0]
    plane = [q for q in range(4) if topo.same_plane(my_chip, topo.chip(cores[q]))][0]
    diag = [q for q in range(4) if q not in (r, mate, plane)][0]
    others = [mate, plane, diag]

    def dst(q):
        a = topo.addr(cores[q])
        return bass.DstId(rid=a[0], pnc=a[1])

    def lidx(sender, receiver):
        return sender if sender < receiver else sender - 1

    def spans(t, u, q0, q1):
        if len(t.shape) == 2:
            return [(q0, q1, t[256 * u + 64 * q0:256 * u + 64 * q1, :])]
        if (q0, q1) == (0, 4):
            return [(0, 4, t[2 * u:2 * u + 2])]
        out = []
        for k in range(2):
            a, b = max(q0, 2 * k), min(q1, 2 * k + 2)
            if b > a:
                out.append((a, b, t[2 * u + k, 64 * (a - 2 * k):64 * (b - 2 * k), :]))
        return out

    def own(t, u):
        return spans(t, u, r, r + 1)[0][2]

    def load(u):
        g.dma_start(T.stg[0:4], spans(T.x, u, 0, 4)[0][2]).then_inc(sm.ld, 16)

    def scatter():
        tr = []
        for q, m, d in ((diag, 0x03, T.land[lidx(r, diag)]), (mate, 0x0C, T.land[lidx(r, mate)]),
                        (plane, 0x30, T.land[lidx(r, plane)]), (plane, 0xC0, T.dup[:])):
            tr.append(bass.RemoteDMATransfer(dst_ids=[dst(q)], dma_engine_mask=m, remote_sem=sm.rs,
                                             src=T.stg[q], dst=d))
        g.remote_dma_fused(tr, local_sem=sm.sn)

    def fold():
        tr = bass.RemoteDMATransfer(dst_ids=[dst(q) for q in others], dma_engine_mask=0xFF, remote_sem=sm.ag,
                                    srcs=[T.stg[r], T.land[0], T.land[1], T.land[2]],
                                    dsts=[T.stg[r] for q in others], alu_op=1)
        g.remote_dma_fused([tr], local_sem=sm.fs)

    def credit():
        tr = [bass.RemoteDMATransfer(dst_ids=[dst(q)], dma_engine_mask=1 << i, remote_sem=sm.cr)
              for i, q in enumerate(others)]
        g.remote_dma_fused(tr, local_sem=sm.sn)

    def add(out, in_, sem):
        g.dma_start(out, in_, accum_op=AluOpType.add, max_dma_last_dim=8192).then_inc(sem, 16)

    def store_others(u):
        n = 0
        for q0, q1 in ((0, r), (r + 1, 4)):
            if q1 > q0:
                for a, b, ap in spans(T.y, u, q0, q1):
                    g.dma_start(ap, T.stg[a:b]).then_inc(sm.cp, 16)
                    n += 16
        return n

    ncp = 0
    load(0)
    for u in range(2):
        g.dma_start(own(T.y, u), own(T.x, u)).then_inc(sm.yo, 16)
    for u in range(2):
        n = u + 1
        g.wait_ge(sm.ld, 16 * n)
        if u:
            g.wait_ge(sm.cr, 3)
        scatter()
        if u == 0:
            g.wait_ge(sm.yo, 32)
        g.wait_ge(sm.rs, 8 * n)
        fold()
        add(own(T.y, u), T.land[lidx(mate, r)], sm.aa)
        add(T.dup[:], T.land[lidx(diag, r)], sm.aa)
        g.wait_ge(sm.aa, 32 * n)
        add(own(T.y, u), T.dup[:], sm.a3)
        g.wait_ge(sm.ag, 24 * n)
        ncp += store_others(u)
        g.wait_ge(sm.fs, 8 * n)
        g.wait_ge(sm.a3, 16 * n)
        if u == 0:
            credit()
            g.wait_ge(sm.cp, ncp)
            g.wait_ge(sm.sn, 11)
            load(1)
    g.wait_ge(sm.cp, ncp)
    g.wait_ge(sm.sn, 19)
